import numpy as np
import ml_dtypes


def mxq(x, axis, fmt="e4m3"):
    dtype, down = {"e4m3": (ml_dtypes.float8_e4m3fn, 7), "e5m2": (ml_dtypes.float8_e5m2, 14)}[fmt]
    v = np.moveaxis(np.asarray(x, np.float32).astype(ml_dtypes.bfloat16).astype(np.float64), axis, -1)
    blocks = v.reshape(v.shape[:-1] + (-1, 32))
    amax = np.abs(blocks).max(-1, keepdims=True)
    byte = np.maximum(np.where(amax > 0, np.frexp(amax)[1] - 1 + 127, 0) - down, 1)
    scale = np.exp2(byte - 127.0)
    codes = (blocks / scale).astype(np.float32).astype(dtype).astype(np.float64)
    return np.moveaxis((codes * scale).reshape(v.shape), -1, axis)


WIDE = False


def mx_kscale(k):
    if not WIDE:
        return np.ones(k)
    levels = np.array([10, -10, 5, -5, 0])
    if k % 512:
        return np.exp2(np.random.permutation(np.resize(levels, k // 32))).repeat(32)
    a = np.empty((k // 512, 16))
    for p in range(k // 512):
        a[p, :8] = np.random.permutation(np.resize(levels, 8))
        for g in range(8):
            far = levels[np.abs(levels - a[p, g]) >= 10]
            a[p, g + 8] = far[np.random.randint(len(far))]
    return np.exp2(a.ravel()).repeat(32)


def f64(x):
    return np.asarray(x).astype(np.float64)


def striped(idx):
    return np.tile(np.asarray(idx).reshape(-1, 16).T, (8, 1)).astype(np.uint16)


def unstriped(offs):
    return offs[:16].T.reshape(-1).astype(np.int64)


def striped8(idx):
    return np.asarray(idx).reshape(8, -1, 16).transpose(0, 2, 1).reshape(128, -1).astype(np.uint16)


def unstriped8(offs):
    return offs.reshape(8, 16, -1).transpose(0, 2, 1).reshape(8, -1).astype(np.int64)


def pick8(x, idx, run):
    r = np.arange(len(x))
    return x[r[:, None], idx[r % (8 * run) // run]]


E2M1 = np.array([0.0, 0.5, 1.0, 1.5, 2.0, 3.0, 4.0, 6.0, -0.0, -0.5, -1.0, -1.5, -2.0, -3.0, -4.0, -6.0])


def pack_weight(w, fmt):
    k, n = w.shape
    w = f64(np.asarray(w, np.float32).astype(ml_dtypes.bfloat16)).reshape(k // 32, 32, n)
    amax = np.abs(w).max(1)
    if fmt == "e4m3":
        byte = np.frexp(amax)[1] - 1 + 127 - 7
    else:
        mant, ex = np.frexp(amax / 6.0)
        byte = np.where(mant > 0.5, ex, ex - 1) + 127
    byte = np.clip(np.where(amax > 0, byte, 1), 1, 254)
    scaled = (w * np.exp2(127.0 - byte)[:, None, :]).reshape(k, n).astype(np.float32)
    by_word = np.ascontiguousarray(scaled.reshape(k // 512, 128, 4, n).transpose(0, 1, 3, 2))
    if fmt == "e4m3":
        words = by_word.astype(ml_dtypes.float8_e4m3fn).view(np.uint8)
    else:
        c = by_word.astype(ml_dtypes.float4_e2m1fn).view(np.uint8) & 0xF
        words = (c[..., 0::2] | (c[..., 1::2] << 4)).reshape(k // 512, 128, 2 * n)
    return np.ascontiguousarray(words), np.ascontiguousarray(byte.astype(np.uint8).reshape(k // 512, 16, n))


def unpack_weight(words, scales, fmt):
    g, _, n = scales.shape
    words = np.ascontiguousarray(words).reshape(g, 128, n, -1)
    if fmt == "e4m3":
        vals = words.view(ml_dtypes.float8_e4m3fn).astype(np.float64)
    else:
        nib = np.empty((g, 128, n, 4), np.uint8)
        nib[..., 0::2] = words & 0xF
        nib[..., 1::2] = words >> 4
        vals = E2M1[nib]
    vals = vals * np.repeat(np.exp2(scales.astype(np.float64) - 127.0), 8, axis=1)[..., None]
    return vals.transpose(0, 1, 3, 2).reshape(g * 512, n)


K, J, R, T, C, D, O, N, S = 512, 256, 512, 1024, 512, 1024, 256, 256, 1024


def setup_inputs():
    n = np.random.standard_normal
    idx = np.random.permutation(T)[:J]
    idx2 = np.stack([np.random.permutation(C)[:J] for _ in range(8)])
    idx3 = np.stack([np.random.permutation(C)[:J] for _ in range(8)])
    idx4 = np.stack([np.random.permutation(D)[:C] for _ in range(8)])
    idx5 = np.stack([np.random.permutation(D)[:O] for _ in range(8)])
    idx6 = np.random.permutation(S)[:N]
    fk = mx_kscale(K)
    fr = mx_kscale(R)
    xtp = pack_weight(n((K, T)) * fk[:, None], "e2m1")
    wp = pack_weight(n((K, R)) * 1 / np.sqrt(K) / fk[:, None] * fr, "e4m3")
    w2p = pack_weight(n((K, R)) * 1 / np.sqrt(K) / fk[:, None] * fr, "e4m3")
    vsp = pack_weight(n((R, S)) * 1 / np.sqrt(R) / fr[:, None], "e2m1")
    return {
        "xt_words": xtp[0],
        "xt_scales": xtp[1],
        "w_words": wp[0],
        "w_scales": wp[1],
        "w2_words": w2p[0],
        "w2_scales": w2p[1],
        "sa": (np.random.uniform(0.5, 1.6, (R, 1))).astype(np.float32),
        "vs_words": vsp[0],
        "vs_scales": vsp[1],
        "offs": striped(idx),
        "offs2": striped8(idx2),
        "offs3": striped8(idx3),
        "offs4": striped8(idx4),
        "offs5": striped8(idx5),
        "offs6": striped(idx6),
    }


def reference(xt_words, xt_scales, w_words, w_scales, w2_words, w2_scales, sa, vs_words, vs_scales, offs, offs2, offs3, offs4, offs5, offs6):
    idx = unstriped(offs)
    idx2 = unstriped8(offs2)
    idx3 = unstriped8(offs3)
    idx4 = unstriped8(offs4)
    idx5 = unstriped8(offs5)
    idx6 = unstriped(offs6)
    xtu = unpack_weight(xt_words, xt_scales, "e2m1")
    wu = unpack_weight(w_words, w_scales, "e4m3")
    w2u = unpack_weight(w2_words, w2_scales, "e4m3")
    vsu = unpack_weight(vs_words, vs_scales, "e2m1")
    xtidxg = xtu[:, idx]
    a = wu.T @ xtidxg
    b = w2u.T @ xtidxg
    pw = np.zeros((R, C))
    pw[np.arange(R)[:, None], idx2[np.arange(R) % 512 // 64]] = a
    pv = np.zeros((R, C))
    pv[np.arange(R)[:, None], idx3[np.arange(R) % 512 // 64]] = b
    pg = pw + pv
    pu = np.zeros((R, D))
    pu[np.arange(R)[:, None], idx4[np.arange(R) % 512 // 64]] = pg
    hid = pick8(pu, idx5, 64) * f64(sa)
    vsidx6g = vsu[:, idx6]
    hidq = mxq(hid, 0, "e4m3")
    y = vsidx6g.T @ hidq
    return y

@@ -1,0 +1,221 @@
+from contextlib import ExitStack
+
+import concourse.mybir as mybir
+
+K, J, R, T, C, D, O, N, S = 512, 256, 512, 1024, 512, 1024, 256, 256, 1024
+FLOPS = 2 * (2 * K * R * J + R * N * O)
+
+F32 = mybir.dt.float32
+BF16 = mybir.dt.bfloat16
+I32 = mybir.dt.int32
+U32 = mybir.dt.uint32
+U16 = mybir.dt.uint16
+U8 = mybir.dt.uint8
+FP8X4 = mybir.dt.float8_e4m3fn_x4
+FP4X4 = mybir.dt.float4_e2m1fn_x4
+COPY = mybir.ActivationFunctionType.Copy
+ADD = mybir.AluOpType.add
+
+P = 128
+PACK = 4
+QUADS = 4
+QUAD = 32
+
+
+def tile_picked_tokens_plain_twin_widened_store_plain_kernel(
+    tc, xt_words, xt_scales, w_words, w_scales, w2_words, w2_scales, sa, vs_words, vs_scales,
+    offs, offs2, offs3, offs4, offs5, offs6, out,
+):
+    nc = tc.nc
+    with ExitStack() as ctx:
+        lists = ctx.enter_context(tc.tile_pool(name="lists", bufs=1))
+        keep = ctx.enter_context(tc.tile_pool(name="keep", bufs=1))
+        psum = ctx.enter_context(tc.psum_pool(name="psum", bufs=1))
+
+        def load_list(src, name):
+            tile = lists.tile(list(src.shape), U16, name=name)
+            nc.sync.dma_start(tile[:], src)
+            return tile
+
+        def load_words(src, dtype, width, name):
+            tile = keep.tile([P, width], dtype, name=name, tag=name, align_bytes=64)
+            nc.sync.dma_start(tile[:].bitcast(I32), src.bitcast(I32))
+            return tile
+
+        def zero_plane(width, name, tag):
+            plane = keep.tile([P, width], U8, name=name, tag=tag, align_bytes=64)
+            nc.vector.memset(plane[:].bitcast(I32), 0)
+            return plane
+
+        def stage_scales(src, name):
+            staged = keep.tile([4, QUADS, src.shape[2] // 4], I32, name=name)
+            nc.sync.dma_start(staged[:], src[0].bitcast(I32).rearrange("(q i) c -> i q c", i=4))
+            return staged
+
+        def spread_scales(staged, plane):
+            for q in range(QUADS):
+                nc.vector.tensor_copy(out=plane[QUAD * q : QUAD * q + 4, :].bitcast(I32), in_=staged[:, q, :])
+
+        def load_scale_rows(queue, src, plane, q):
+            queue.dma_start(
+                plane[QUAD * q : QUAD * q + 4, :].bitcast(I32), src[0, 4 * q : 4 * q + 4, :].bitcast(I32)
+            )
+
+        def load_scales(src, plane):
+            for q in range(QUADS):
+                load_scale_rows(nc.sync, src, plane, q)
+
+        def flat_words(src):
+            return src[0].rearrange("p c j -> p (c j)")
+
+        def zero_board(width, name, tag):
+            board = keep.tile([P, width], F32, name=name, tag=tag, align_bytes=64)
+            nc.vector.memset(board[:], 0.0)
+            return board
+
+        xs_table = zero_plane(T, "xs_table", "xs_table")
+        for q in range(QUADS - 1):
+            load_scale_rows(nc.scalar, xt_scales, xs_table, q)
+        ws_staged = stage_scales(w_scales, "ws_staged")
+        xt_table = load_words(xt_words[0], U16, T, "xt_table")
+        load_scale_rows(nc.sync, xt_scales, xs_table, QUADS - 1)
+        idx = load_list(offs, "idx")
+        w_raw = load_words(flat_words(w_words), I32, R, "w_raw")
+        idx2 = load_list(offs2, "idx2")
+        ws_raw = zero_plane(R, "ws_raw", "ws_raw")
+        w2s_raw = zero_plane(R, "w2s_raw", "w2s_raw")
+        pw = [zero_board(C, "pw0", "pw0"), zero_board(C, "pw1", "pw1")]
+        pv = [zero_board(C, "pv0", "pv0")]
+        w2_raw = load_words(flat_words(w2_words), I32, R, "w2_raw")
+        load_scales(w2_scales, w2s_raw)
+        idx3 = load_list(offs3, "idx3")
+        idx4 = load_list(offs4, "idx4")
+        idx5 = load_list(offs5, "idx5")
+        sa_sb = keep.tile([P, PACK], F32)
+        nc.sync.dma_start(sa_sb[:], sa.rearrange("(p t) o -> p (t o)", t=PACK))
+        idx6 = load_list(offs6, "idx6")
+        vs_table = load_words(vs_words[0], U16, S, "vs_table")
+
+        spread_scales(ws_staged, ws_raw)
+
+        def deal(raw, dtype, ts, tag):
+            dealt = keep.tile([P, len(ts), P], dtype, name="dealt", tag=tag, align_bytes=64)
+            nc.vector.tensor_copy(
+                out=dealt[:], in_=raw[:].rearrange("p (m t) -> p t m", t=PACK)[:, ts.start : ts.stop, :]
+            )
+            return dealt
+
+        def gather(table, offsets, dtype, name):
+            picked = keep.tile([P, J], dtype, name=name, align_bytes=64)
+            nc.vector.tensor_copy(out=picked[:], in_=table[:].indirect(offsets[:]))
+            return picked
+
+        def multiply(words, scales):
+            acc = psum.tile([P, J], F32, name="acc", bufs=6)
+            nc.tensor.matmul_mx(
+                out=acc[:], lhsT=words.bitcast(FP8X4), lhsT_scale=scales,
+                rhs=xw[:].bitcast(FP4X4), rhs_scale=xs[:], start=True, stop=True,
+            )
+            return acc
+
+        def products(raw, raw_scales, ts, name, tags):
+            scales = deal(raw_scales, U8, ts, tags[0])
+            words = deal(raw, I32, ts, tags[1])
+            results = {}
+            for i, t in enumerate(ts):
+                results[t] = keep.tile([P, J], F32, name="%s%d" % (name, t))
+                nc.vector.tensor_copy(out=results[t][:], in_=multiply(words[:, i, :], scales[:, i, :])[:])
+            return results
+
+        def scatter(board, offsets, values):
+            nc.scalar.activation(out=board[:].indirect(offsets), in_=values, func=COPY)
+
+        hid = keep.tile([P, PACK, O], BF16, align_bytes=64)
+        pg = {}
+
+        def add_boards(t, tag):
+            pg[t] = keep.tile([P, C], F32, name="pg%d" % t, tag=tag, align_bytes=64)
+            nc.vector.tensor_tensor(out=pg[t][:], in0=pw[t % 2][:], in1=pv[t % 2][:], op=ADD)
+
+        def widen(t):
+            scatter(pu[t % 2], idx4[:], pg[t][:])
+
+        HALF = O // 2
+
+        def fetch(t):
+            nc.scalar.activation(
+                out=hid[:, t, :], in_=pu[t % 2][:].indirect(idx5[:]), func=COPY, scale=sa_sb[:, t : t + 1]
+            )
+
+        def weave(planes):
+            for h in range(2):
+                nc.vector.tensor_copy(
+                    out=grouped[h][:, :, planes],
+                    in_=hid[:, planes, h * HALF : (h + 1) * HALF].rearrange("p t c -> p c t"),
+                )
+
+        ws0 = deal(ws_raw, U8, range(0, 1), "a_s0")
+        xw = gather(xt_table, idx, U16, "xw")
+        xs = gather(xs_table, idx, U8, "xs")
+        w0 = deal(w_raw, I32, range(0, 1), "a_w0")
+        a = {0: keep.tile([P, J], F32, name="a0")}
+        nc.scalar.activation(out=a[0][:], in_=multiply(w0[:, 0, :], ws0[:, 0, :])[:], func=COPY)
+        scatter(pw[0], idx2[:], a[0][:])
+        a = {**a, **products(w_raw, ws_raw, range(1, 2), "a", ("xs_table", "xt_table"))}
+        scatter(pw[1], idx2[:], a[1][:])
+        pv.append(zero_board(C, "pv1", "xt_table"))
+        b = {}
+        for t in (0, 1):
+            b = {**b, **products(w2_raw, w2s_raw, range(t, t + 1), "b", ("s%d" % t, "w%d" % t))}
+            scatter(pv[t], idx3[:], b[t][:])
+        pu = [zero_board(D, "pu0", "w1")]
+        add_boards(0, "s1")
+        widen(0)
+        a = {**a, **products(w_raw, ws_raw, range(2, 4), "a", ("s0", "w0"))}
+        b = {**b, **products(w2_raw, w2s_raw, range(2, 4), "b", ("s0", "w0"))}
+        add_boards(1, "s0")
+        pu.append(zero_board(D, "pu1", "w2_raw"))
+        scatter(pw[0], idx2[:], a[2][:])
+        scatter(pv[0], idx3[:], b[2][:])
+        add_boards(2, "w0")
+        widen(1)
+        fetch(0)
+        vss_table = zero_plane(S, "vss_table", "ws_raw")
+        load_scales(vs_scales, vss_table)
+        vsw = gather(vs_table, idx6, U16, "vsw")
+        vss = gather(vss_table, idx6, U8, "vss")
+        scatter(pw[1], idx2[:], a[3][:])
+        scatter(pv[1], idx3[:], b[3][:])
+        add_boards(3, "pg3")
+        widen(2)
+        fetch(1)
+        grouped = [
+            keep.tile([P, HALF, PACK], BF16, name="grouped", tag=tag, align_bytes=64)
+            for tag in ("ws_raw", "vs_table")
+        ]
+        weave(slice(0, 2))
+        widen(3)
+        fetch(2)
+        weave(slice(2, 3))
+        fetch(3)
+        weave(slice(3, 4))
+        out_view = out.rearrange("(u p) o -> p u o", p=P)
+        for h in range(2):
+            codes = keep.tile([P, HALF], U32, name="codes%d" % h, align_bytes=64)
+            scales = keep.tile([P, HALF], U8, name="scales%d" % h, align_bytes=64)
+            nc.vector.quantize_mx(
+                out=codes[:].bitcast(FP8X4), scales=scales[:], in_=grouped[h][:].rearrange("p c t -> p (c t)")
+            )
+            y = psum.tile([P, 2, HALF], F32, name="y%d" % h)
+            for u in range(2):
+                nc.tensor.matmul_mx(
+                    out=y[:, u, :], lhsT=vsw[:, u * P : (u + 1) * P].bitcast(FP4X4), lhsT_scale=vss[:, u * P : (u + 1) * P],
+                    rhs=codes[:].bitcast(FP8X4), rhs_scale=scales[:], start=True, stop=True,
+                )
+            y_sb = keep.tile([P, 2, HALF], F32, name="y_sb%d" % h)
+            if h == 0:
+                nc.vector.tensor_copy(out=y_sb[:], in_=y[:])
+                nc.sync.dma_start(out_view[:, :, 0:HALF], y_sb[:])
+            else:
+                nc.scalar.copy(out=y_sb[:], in_=y[:])
+                nc.scalar.dma_start(out_view[:, :, HALF:O], y_sb[:])

@@ -49,7 +49,7 @@ def tile_picked_tokens_plain_twin_widened_store_plain_kernel(
 
         def stage_scales(src, name):
             staged = keep.tile([4, QUADS, src.shape[2] // 4], I32, name=name)
-            nc.sync.dma_start(staged[:], src[0].bitcast(I32).rearrange("(q i) c -> i q c", i=4))
+            nc.scalar.dma_start(staged[:], src[0].bitcast(I32).rearrange("(q i) c -> i q c", i=4))
             return staged
 
         def spread_scales(staged, plane):
@@ -73,19 +73,18 @@ def tile_picked_tokens_plain_twin_widened_store_plain_kernel(
             nc.vector.memset(board[:], 0.0)
             return board
 
+        ws_staged = stage_scales(w_scales, "ws_staged")
         xs_table = zero_plane(T, "xs_table", "xs_table")
         for q in range(QUADS - 1):
             load_scale_rows(nc.scalar, xt_scales, xs_table, q)
-        ws_staged = stage_scales(w_scales, "ws_staged")
-        xt_table = load_words(xt_words[0], U16, T, "xt_table")
-        load_scale_rows(nc.sync, xt_scales, xs_table, QUADS - 1)
-        idx = load_list(offs, "idx")
         w_raw = load_words(flat_words(w_words), I32, R, "w_raw")
+        load_scale_rows(nc.sync, xt_scales, xs_table, QUADS - 1)
+        xt_table = load_words(xt_words[0], U16, T, "xt_table")
+        idx = load_list(offs, "idx")
         idx2 = load_list(offs2, "idx2")
         ws_raw = zero_plane(R, "ws_raw", "ws_raw")
         w2s_raw = zero_plane(R, "w2s_raw", "w2s_raw")
         pw = [zero_board(C, "pw0", "pw0"), zero_board(C, "pw1", "pw1")]
-        pv = [zero_board(C, "pv0", "pv0")]
         w2_raw = load_words(flat_words(w2_words), I32, R, "w2_raw")
         load_scales(w2_scales, w2s_raw)
         idx3 = load_list(offs3, "idx3")
@@ -101,20 +100,24 @@ def tile_picked_tokens_plain_twin_widened_store_plain_kernel(
         def deal(raw, dtype, ts, tag):
             dealt = keep.tile([P, len(ts), P], dtype, name="dealt", tag=tag, align_bytes=64)
             nc.vector.tensor_copy(
-                out=dealt[:], in_=raw[:].rearrange("p (m t) -> p t m", t=PACK)[:, ts.start : ts.stop, :]
+                out=dealt[:].rearrange("p t m -> p m t"),
+                in_=raw[:].rearrange("p (m t) -> p m t", t=PACK)[:, :, ts.start : ts.stop],
             )
             return dealt
 
-        def gather(table, offsets, dtype, name):
-            picked = keep.tile([P, J], dtype, name=name, align_bytes=64)
-            nc.vector.tensor_copy(out=picked[:], in_=table[:].indirect(offsets[:]))
-            return picked
+        def gather(picked, table, offsets, cols):
+            nc.vector.tensor_copy(
+                out=picked[:, cols], in_=table[:].indirect(offsets[:, cols.start // 16 : cols.stop // 16])
+            )
 
-        def multiply(words, scales):
-            acc = psum.tile([P, J], F32, name="acc", bufs=6)
+        xw = keep.tile([P, J], U16, align_bytes=64)
+        xs = keep.tile([P, J], U8, align_bytes=64)
+
+        def multiply(words, scales, cols, bank, bufs):
+            acc = psum.tile([P, cols.stop - cols.start], F32, name="acc", tag=bank, bufs=bufs)
             nc.tensor.matmul_mx(
                 out=acc[:], lhsT=words.bitcast(FP8X4), lhsT_scale=scales,
-                rhs=xw[:].bitcast(FP4X4), rhs_scale=xs[:], start=True, stop=True,
+                rhs=xw[:, cols].bitcast(FP4X4), rhs_scale=xs[:, cols], start=True, stop=True,
             )
             return acc
 
@@ -124,81 +127,84 @@ def tile_picked_tokens_plain_twin_widened_store_plain_kernel(
             results = {}
             for i, t in enumerate(ts):
                 results[t] = keep.tile([P, J], F32, name="%s%d" % (name, t))
-                nc.vector.tensor_copy(out=results[t][:], in_=multiply(words[:, i, :], scales[:, i, :])[:])
+                nc.vector.tensor_copy(out=results[t][:], in_=multiply(words[:, i, :], scales[:, i, :], slice(0, J), "acc", 5)[:])
             return results
 
         def scatter(board, offsets, values):
             nc.scalar.activation(out=board[:].indirect(offsets), in_=values, func=COPY)
 
-        hid = keep.tile([P, PACK, O], BF16, align_bytes=64)
+        hid = {}
         pg = {}
 
         def add_boards(t, tag):
             pg[t] = keep.tile([P, C], F32, name="pg%d" % t, tag=tag, align_bytes=64)
-            nc.vector.tensor_tensor(out=pg[t][:], in0=pw[t % 2][:], in1=pv[t % 2][:], op=ADD)
+            nc.vector.tensor_tensor(out=pg[t][:], in0=pw[t][:], in1=pv[t % 2][:], op=ADD)
 
         def widen(t):
             scatter(pu[t % 2], idx4[:], pg[t][:])
 
         HALF = O // 2
 
-        def fetch(t):
+        def fetch(t, tag):
+            hid[t] = keep.tile([P, O], BF16, name="hid%d" % t, tag=tag, align_bytes=64)
             nc.scalar.activation(
-                out=hid[:, t, :], in_=pu[t % 2][:].indirect(idx5[:]), func=COPY, scale=sa_sb[:, t : t + 1]
+                out=hid[t][:], in_=pu[t % 2][:].indirect(idx5[:]), func=COPY, scale=sa_sb[:, t : t + 1]
             )
 
-        def weave(planes):
+        def weave(t):
             for h in range(2):
-                nc.vector.tensor_copy(
-                    out=grouped[h][:, :, planes],
-                    in_=hid[:, planes, h * HALF : (h + 1) * HALF].rearrange("p t c -> p c t"),
-                )
+                nc.vector.tensor_copy(out=grouped[h][:, :, t], in_=hid[t][:, h * HALF : (h + 1) * HALF])
 
-        ws0 = deal(ws_raw, U8, range(0, 1), "a_s0")
-        xw = gather(xt_table, idx, U16, "xw")
-        xs = gather(xs_table, idx, U8, "xs")
-        w0 = deal(w_raw, I32, range(0, 1), "a_w0")
-        a = {0: keep.tile([P, J], F32, name="a0")}
-        nc.scalar.activation(out=a[0][:], in_=multiply(w0[:, 0, :], ws0[:, 0, :])[:], func=COPY)
-        scatter(pw[0], idx2[:], a[0][:])
-        a = {**a, **products(w_raw, ws_raw, range(1, 2), "a", ("xs_table", "xt_table"))}
-        scatter(pw[1], idx2[:], a[1][:])
-        pv.append(zero_board(C, "pv1", "xt_table"))
-        b = {}
+        first = [(deal(ws_raw, U8, range(t, t + 1), "a_s%d" % t), deal(w_raw, I32, range(t, t + 1), "a_w%d" % t)) for t in (0, 1)]
+        halves = [slice(0, J // 2), slice(J // 2, J)]
+        for cols in halves:
+            gather(xw, xt_table, idx, cols)
+            gather(xs, xs_table, idx, cols)
+        a0 = [keep.tile([P, J // 2], F32, name="a0_%d" % h) for h in range(2)]
+        a1 = keep.tile([P, J], F32)
+        nc.scalar.activation(out=a0[0][:], in_=multiply(first[0][1][:, 0, :], first[0][0][:, 0, :], halves[0], "head", 1)[:], func=COPY)
+        scatter(pw[0], idx2[:, 0:8], a0[0][:])
+        nc.vector.tensor_copy(out=a0[1][:], in_=multiply(first[0][1][:, 0, :], first[0][0][:, 0, :], halves[1], "acc", 5)[:])
+        scatter(pw[0], idx2[:, 8:16], a0[1][:])
+        nc.vector.tensor_copy(out=a1[:], in_=multiply(first[1][1][:, 0, :], first[1][0][:, 0, :], slice(0, J), "head", 1)[:])
+        scatter(pw[1], idx2[:], a1[:])
+        pw.append(zero_board(C, "pw2", "xt_table"))
+        pw.append(zero_board(C, "pw3", "xs_table"))
+        a = products(w_raw, ws_raw, range(2, 4), "a", ("a_s1", "a_w1"))
+        for t in (2, 3):
+            scatter(pw[t], idx2[:], a[t][:])
+        b = products(w2_raw, w2s_raw, range(0, 4), "b", ("a_s1", "a_w1"))
+        pv = [zero_board(C, "pv0", "w2s_raw"), zero_board(C, "pv1", "w2_raw")]
         for t in (0, 1):
-            b = {**b, **products(w2_raw, w2s_raw, range(t, t + 1), "b", ("s%d" % t, "w%d" % t))}
             scatter(pv[t], idx3[:], b[t][:])
-        pu = [zero_board(D, "pu0", "w1")]
-        add_boards(0, "s1")
+        pu = [zero_board(D, "pu0", "a_w1")]
+        add_boards(0, "a_s1")
         widen(0)
-        a = {**a, **products(w_raw, ws_raw, range(2, 4), "a", ("s0", "w0"))}
-        b = {**b, **products(w2_raw, w2s_raw, range(2, 4), "b", ("s0", "w0"))}
-        add_boards(1, "s0")
-        pu.append(zero_board(D, "pu1", "w2_raw"))
-        scatter(pw[0], idx2[:], a[2][:])
+        pu.append(zero_board(D, "pu1", "pw0"))
+        add_boards(1, "pg1")
         scatter(pv[0], idx3[:], b[2][:])
-        add_boards(2, "w0")
+        add_boards(2, "pg2")
+        fetch(0, "hid0")
         widen(1)
-        fetch(0)
-        vss_table = zero_plane(S, "vss_table", "ws_raw")
-        load_scales(vs_scales, vss_table)
-        vsw = gather(vs_table, idx6, U16, "vsw")
-        vss = gather(vss_table, idx6, U8, "vss")
-        scatter(pw[1], idx2[:], a[3][:])
         scatter(pv[1], idx3[:], b[3][:])
         add_boards(3, "pg3")
+        fetch(1, "hid1")
         widen(2)
-        fetch(1)
+        widen(3)
+        fetch(2, "xs_table")
+        fetch(3, "hid3")
+        vss_table = zero_plane(S, "vss_table", "ws_raw")
+        load_scales(vs_scales, vss_table)
+        vsw = keep.tile([P, N], U16, tag="pw1", align_bytes=64)
+        vss = keep.tile([P, N], U8, align_bytes=64)
+        gather(vsw, vs_table, idx6, slice(0, N))
+        gather(vss, vss_table, idx6, slice(0, N))
         grouped = [
             keep.tile([P, HALF, PACK], BF16, name="grouped", tag=tag, align_bytes=64)
             for tag in ("ws_raw", "vs_table")
         ]
-        weave(slice(0, 2))
-        widen(3)
-        fetch(2)
-        weave(slice(2, 3))
-        fetch(3)
-        weave(slice(3, 4))
+        for t in range(PACK):
+            weave(t)
         out_view = out.rearrange("(u p) o -> p u o", p=P)
         for h in range(2):
             codes = keep.tile([P, HALF], U32, name="codes%d" % h, align_bytes=64)

from contextlib import ExitStack

import concourse.mybir as mybir

K, J, R, T, C, D, O, N, S = 512, 256, 512, 1024, 512, 1024, 256, 256, 1024
FLOPS = 2 * (2 * K * R * J + R * N * O)

F32 = mybir.dt.float32
BF16 = mybir.dt.bfloat16
I32 = mybir.dt.int32
U32 = mybir.dt.uint32
U16 = mybir.dt.uint16
U8 = mybir.dt.uint8
FP8X4 = mybir.dt.float8_e4m3fn_x4
FP4X4 = mybir.dt.float4_e2m1fn_x4
COPY = mybir.ActivationFunctionType.Copy
ADD = mybir.AluOpType.add

P = 128
PACK = 4
QUADS = 4
QUAD = 32


def tile_picked_tokens_plain_twin_widened_store_plain_kernel(
    tc, xt_words, xt_scales, w_words, w_scales, w2_words, w2_scales, sa, vs_words, vs_scales,
    offs, offs2, offs3, offs4, offs5, offs6, out,
):
    nc = tc.nc
    with ExitStack() as ctx:
        lists = ctx.enter_context(tc.tile_pool(name="lists", bufs=1))
        keep = ctx.enter_context(tc.tile_pool(name="keep", bufs=1))
        psum = ctx.enter_context(tc.psum_pool(name="psum", bufs=1))

        def load_list(src, name):
            tile = lists.tile(list(src.shape), U16, name=name)
            nc.sync.dma_start(tile[:], src)
            return tile

        def load_words(src, dtype, width, name):
            tile = keep.tile([P, width], dtype, name=name, tag=name, align_bytes=64)
            nc.sync.dma_start(tile[:].bitcast(I32), src.bitcast(I32))
            return tile

        def zero_plane(width, name, tag):
            plane = keep.tile([P, width], U8, name=name, tag=tag, align_bytes=64)
            nc.vector.memset(plane[:].bitcast(I32), 0)
            return plane

        def stage_scales(src, name):
            staged = keep.tile([4, QUADS, src.shape[2] // 4], I32, name=name)
            nc.scalar.dma_start(staged[:], src[0].bitcast(I32).rearrange("(q i) c -> i q c", i=4))
            return staged

        def spread_scales(staged, plane):
            for q in range(QUADS):
                nc.vector.tensor_copy(out=plane[QUAD * q : QUAD * q + 4, :].bitcast(I32), in_=staged[:, q, :])

        def load_scale_rows(queue, src, plane, q):
            queue.dma_start(
                plane[QUAD * q : QUAD * q + 4, :].bitcast(I32), src[0, 4 * q : 4 * q + 4, :].bitcast(I32)
            )

        def load_scales(src, plane):
            for q in range(QUADS):
                load_scale_rows(nc.sync, src, plane, q)

        def flat_words(src):
            return src[0].rearrange("p c j -> p (c j)")

        def zero_board(width, name, tag):
            board = keep.tile([P, width], F32, name=name, tag=tag, align_bytes=64)
            nc.vector.memset(board[:], 0.0)
            return board

        ws_staged = stage_scales(w_scales, "ws_staged")
        xs_table = zero_plane(T, "xs_table", "xs_table")
        for q in range(QUADS - 1):
            load_scale_rows(nc.scalar, xt_scales, xs_table, q)
        w_raw = load_words(flat_words(w_words), I32, R, "w_raw")
        load_scale_rows(nc.sync, xt_scales, xs_table, QUADS - 1)
        xt_table = load_words(xt_words[0], U16, T, "xt_table")
        idx = load_list(offs, "idx")
        idx2 = load_list(offs2, "idx2")
        ws_raw = zero_plane(R, "ws_raw", "ws_raw")
        w2s_raw = zero_plane(R, "w2s_raw", "w2s_raw")
        pw = [zero_board(C, "pw0", "pw0"), zero_board(C, "pw1", "pw1")]
        w2_raw = load_words(flat_words(w2_words), I32, R, "w2_raw")
        load_scales(w2_scales, w2s_raw)
        idx3 = load_list(offs3, "idx3")
        idx4 = load_list(offs4, "idx4")
        idx5 = load_list(offs5, "idx5")
        sa_sb = keep.tile([P, PACK], F32)
        nc.sync.dma_start(sa_sb[:], sa.rearrange("(p t) o -> p (t o)", t=PACK))
        idx6 = load_list(offs6, "idx6")
        vs_table = load_words(vs_words[0], U16, S, "vs_table")

        spread_scales(ws_staged, ws_raw)

        def deal(raw, dtype, ts, tag):
            dealt = keep.tile([P, len(ts), P], dtype, name="dealt", tag=tag, align_bytes=64)
            nc.vector.tensor_copy(
                out=dealt[:].rearrange("p t m -> p m t"),
                in_=raw[:].rearrange("p (m t) -> p m t", t=PACK)[:, :, ts.start : ts.stop],
            )
            return dealt

        def gather(picked, table, offsets, cols):
            nc.vector.tensor_copy(
                out=picked[:, cols], in_=table[:].indirect(offsets[:, cols.start // 16 : cols.stop // 16])
            )

        xw = keep.tile([P, J], U16, align_bytes=64)
        xs = keep.tile([P, J], U8, align_bytes=64)

        def multiply(words, scales, cols, bank, bufs):
            acc = psum.tile([P, cols.stop - cols.start], F32, name="acc", tag=bank, bufs=bufs)
            nc.tensor.matmul_mx(
                out=acc[:], lhsT=words.bitcast(FP8X4), lhsT_scale=scales,
                rhs=xw[:, cols].bitcast(FP4X4), rhs_scale=xs[:, cols], start=True, stop=True,
            )
            return acc

        def products(raw, raw_scales, ts, name, tags):
            scales = deal(raw_scales, U8, ts, tags[0])
            words = deal(raw, I32, ts, tags[1])
            results = {}
            for i, t in enumerate(ts):
                results[t] = keep.tile([P, J], F32, name="%s%d" % (name, t))
                nc.vector.tensor_copy(out=results[t][:], in_=multiply(words[:, i, :], scales[:, i, :], slice(0, J), "acc", 5)[:])
            return results

        def scatter(board, offsets, values):
            nc.scalar.activation(out=board[:].indirect(offsets), in_=values, func=COPY)

        hid = {}
        pg = {}

        def add_boards(t, tag):
            pg[t] = keep.tile([P, C], F32, name="pg%d" % t, tag=tag, align_bytes=64)
            nc.vector.tensor_tensor(out=pg[t][:], in0=pw[t][:], in1=pv[t % 2][:], op=ADD)

        def widen(t):
            scatter(pu[t % 2], idx4[:], pg[t][:])

        HALF = O // 2

        def fetch(t, tag):
            hid[t] = keep.tile([P, O], BF16, name="hid%d" % t, tag=tag, align_bytes=64)
            nc.scalar.activation(
                out=hid[t][:], in_=pu[t % 2][:].indirect(idx5[:]), func=COPY, scale=sa_sb[:, t : t + 1]
            )

        def weave(t):
            for h in range(2):
                nc.vector.tensor_copy(out=grouped[h][:, :, t], in_=hid[t][:, h * HALF : (h + 1) * HALF])

        first = [(deal(ws_raw, U8, range(t, t + 1), "a_s%d" % t), deal(w_raw, I32, range(t, t + 1), "a_w%d" % t)) for t in (0, 1)]
        halves = [slice(0, J // 2), slice(J // 2, J)]
        for cols in halves:
            gather(xw, xt_table, idx, cols)
            gather(xs, xs_table, idx, cols)
        a0 = [keep.tile([P, J // 2], F32, name="a0_%d" % h) for h in range(2)]
        a1 = keep.tile([P, J], F32)
        nc.scalar.activation(out=a0[0][:], in_=multiply(first[0][1][:, 0, :], first[0][0][:, 0, :], halves[0], "head", 1)[:], func=COPY)
        scatter(pw[0], idx2[:, 0:8], a0[0][:])
        nc.vector.tensor_copy(out=a0[1][:], in_=multiply(first[0][1][:, 0, :], first[0][0][:, 0, :], halves[1], "acc", 5)[:])
        scatter(pw[0], idx2[:, 8:16], a0[1][:])
        nc.vector.tensor_copy(out=a1[:], in_=multiply(first[1][1][:, 0, :], first[1][0][:, 0, :], slice(0, J), "head", 1)[:])
        scatter(pw[1], idx2[:], a1[:])
        pw.append(zero_board(C, "pw2", "xt_table"))
        pw.append(zero_board(C, "pw3", "xs_table"))
        a = products(w_raw, ws_raw, range(2, 4), "a", ("a_s1", "a_w1"))
        for t in (2, 3):
            scatter(pw[t], idx2[:], a[t][:])
        b = products(w2_raw, w2s_raw, range(0, 4), "b", ("a_s1", "a_w1"))
        pv = [zero_board(C, "pv0", "w2s_raw"), zero_board(C, "pv1", "w2_raw")]
        for t in (0, 1):
            scatter(pv[t], idx3[:], b[t][:])
        pu = [zero_board(D, "pu0", "a_w1")]
        add_boards(0, "a_s1")
        widen(0)
        pu.append(zero_board(D, "pu1", "pw0"))
        add_boards(1, "pg1")
        scatter(pv[0], idx3[:], b[2][:])
        add_boards(2, "pg2")
        fetch(0, "hid0")
        widen(1)
        scatter(pv[1], idx3[:], b[3][:])
        add_boards(3, "pg3")
        fetch(1, "hid1")
        widen(2)
        widen(3)
        fetch(2, "xs_table")
        fetch(3, "hid3")
        vss_table = zero_plane(S, "vss_table", "ws_raw")
        load_scales(vs_scales, vss_table)
        vsw = keep.tile([P, N], U16, tag="pw1", align_bytes=64)
        vss = keep.tile([P, N], U8, align_bytes=64)
        gather(vsw, vs_table, idx6, slice(0, N))
        gather(vss, vss_table, idx6, slice(0, N))
        grouped = [
            keep.tile([P, HALF, PACK], BF16, name="grouped", tag=tag, align_bytes=64)
            for tag in ("ws_raw", "vs_table")
        ]
        for t in range(PACK):
            weave(t)
        out_view = out.rearrange("(u p) o -> p u o", p=P)
        for h in range(2):
            codes = keep.tile([P, HALF], U32, name="codes%d" % h, align_bytes=64)
            scales = keep.tile([P, HALF], U8, name="scales%d" % h, align_bytes=64)
            nc.vector.quantize_mx(
                out=codes[:].bitcast(FP8X4), scales=scales[:], in_=grouped[h][:].rearrange("p c t -> p (c t)")
            )
            y = psum.tile([P, 2, HALF], F32, name="y%d" % h)
            for u in range(2):
                nc.tensor.matmul_mx(
                    out=y[:, u, :], lhsT=vsw[:, u * P : (u + 1) * P].bitcast(FP4X4), lhsT_scale=vss[:, u * P : (u + 1) * P],
                    rhs=codes[:].bitcast(FP8X4), rhs_scale=scales[:], start=True, stop=True,
                )
            y_sb = keep.tile([P, 2, HALF], F32, name="y_sb%d" % h)
            if h == 0:
                nc.vector.tensor_copy(out=y_sb[:], in_=y[:])
                nc.sync.dma_start(out_view[:, :, 0:HALF], y_sb[:])
            else:
                nc.scalar.copy(out=y_sb[:], in_=y[:])
                nc.scalar.dma_start(out_view[:, :, HALF:O], y_sb[:])
